import numpy as np
import ml_dtypes


def mxq(x, axis, fmt="e4m3"):
    dtype, down = {"e4m3": (ml_dtypes.float8_e4m3fn, 7), "e5m2": (ml_dtypes.float8_e5m2, 14)}[fmt]
    v = np.moveaxis(np.asarray(x, np.float32).astype(ml_dtypes.bfloat16).astype(np.float64), axis, -1)
    blocks = v.reshape(v.shape[:-1] + (-1, 32))
    amax = np.abs(blocks).max(-1, keepdims=True)
    byte = np.maximum(np.where(amax > 0, np.frexp(amax)[1] - 1 + 127, 0) - down, 1)
    scale = np.exp2(byte - 127.0)
    codes = (blocks / scale).astype(np.float32).astype(dtype).astype(np.float64)
    return np.moveaxis((codes * scale).reshape(v.shape), -1, axis)


WIDE = False


def mx_kscale(k):
    if not WIDE:
        return np.ones(k)
    levels = np.array([10, -10, 5, -5, 0])
    if k % 512:
        return np.exp2(np.random.permutation(np.resize(levels, k // 32))).repeat(32)
    a = np.empty((k // 512, 16))
    for p in range(k // 512):
        a[p, :8] = np.random.permutation(np.resize(levels, 8))
        for g in range(8):
            far = levels[np.abs(levels - a[p, g]) >= 10]
            a[p, g + 8] = far[np.random.randint(len(far))]
    return np.exp2(a.ravel()).repeat(32)


def f64(x):
    return np.asarray(x).astype(np.float64)


def striped(idx):
    return np.tile(np.asarray(idx).reshape(-1, 16).T, (8, 1)).astype(np.uint16)


def unstriped(offs):
    return offs[:16].T.reshape(-1).astype(np.int64)


E2M1 = np.array([0.0, 0.5, 1.0, 1.5, 2.0, 3.0, 4.0, 6.0, -0.0, -0.5, -1.0, -1.5, -2.0, -3.0, -4.0, -6.0])


def pack_weight(w, fmt):
    k, n = w.shape
    w = f64(np.asarray(w, np.float32).astype(ml_dtypes.bfloat16)).reshape(k // 32, 32, n)
    amax = np.abs(w).max(1)
    if fmt == "e4m3":
        byte = np.frexp(amax)[1] - 1 + 127 - 7
    else:
        mant, ex = np.frexp(amax / 6.0)
        byte = np.where(mant > 0.5, ex, ex - 1) + 127
    byte = np.clip(np.where(amax > 0, byte, 1), 1, 254)
    scaled = (w * np.exp2(127.0 - byte)[:, None, :]).reshape(k, n).astype(np.float32)
    by_word = np.ascontiguousarray(scaled.reshape(k // 512, 128, 4, n).transpose(0, 1, 3, 2))
    if fmt == "e4m3":
        words = by_word.astype(ml_dtypes.float8_e4m3fn).view(np.uint8)
    else:
        c = by_word.astype(ml_dtypes.float4_e2m1fn).view(np.uint8) & 0xF
        words = (c[..., 0::2] | (c[..., 1::2] << 4)).reshape(k // 512, 128, 2 * n)
    return np.ascontiguousarray(words), np.ascontiguousarray(byte.astype(np.uint8).reshape(k // 512, 16, n))


def unpack_weight(words, scales, fmt):
    g, _, n = scales.shape
    words = np.ascontiguousarray(words).reshape(g, 128, n, -1)
    if fmt == "e4m3":
        vals = words.view(ml_dtypes.float8_e4m3fn).astype(np.float64)
    else:
        nib = np.empty((g, 128, n, 4), np.uint8)
        nib[..., 0::2] = words & 0xF
        nib[..., 1::2] = words >> 4
        vals = E2M1[nib]
    vals = vals * np.repeat(np.exp2(scales.astype(np.float64) - 127.0), 8, axis=1)[..., None]
    return vals.transpose(0, 1, 3, 2).reshape(g * 512, n)


D, E, T, I, Q = 512, 512, 2048, 512, 128


def setup_inputs():
    n = np.random.standard_normal
    idx = np.random.permutation(T)[:I]
    fd = mx_kscale(D)
    fe = mx_kscale(E)
    keysp = pack_weight(n((D, T)) / fd[:, None], "e4m3")
    valsp = pack_weight(n((E, T)) / fe[:, None], "e4m3")
    return {
        "query": (n((D, Q)) * 1.0 / np.sqrt(D) * fd[:, None]).astype(np.float32),
        "query2": (n((D, Q)) * 1.0 / np.sqrt(D) * fd[:, None]).astype(np.float32),
        "keys_words": keysp[0],
        "keys_scales": keysp[1],
        "prior1": np.tile(np.random.uniform(0.1, 0.9, T), (128, 1)).astype(np.float32),
        "lam": (np.random.uniform(0.7, 1.4, (Q, 1))).astype(np.float32),
        "gout": (n((E, Q)) * 1 / np.sqrt(E) * fe[:, None]).astype(np.float32),
        "vals_words": valsp[0],
        "vals_scales": valsp[1],
        "dquery": (n((D, Q)) * 1.0 / np.sqrt(D) * fd[:, None]).astype(np.float32),
        "base": (0.5 * n((Q, T))).astype(np.float32),
        "offs": striped(idx),
    }


def reference(query, query2, keys_words, keys_scales, prior1, lam, gout, vals_words, vals_scales, dquery, base, offs):
    idx = unstriped(offs)
    keysu = unpack_weight(keys_words, keys_scales, "e4m3")
    valsu = unpack_weight(vals_words, vals_scales, "e4m3")
    queryq = mxq(f64(query), 0, "e4m3")
    keysidxg = keysu[:, idx]
    a = queryq.T @ keysidxg
    dqueryq = mxq(f64(dquery), 0, "e4m3")
    ta = dqueryq.T @ keysidxg
    query2q = mxq(f64(query2), 0, "e4m3")
    b = query2q.T @ keysidxg
    ea = np.exp(a) * f64(prior1)[:1][:, idx]
    eb = np.exp(b) * (1.0 - f64(prior1)[:1][:, idx])
    s = np.log(ea + eb) * f64(lam)
    p = np.exp(s - np.max(s, axis=1, keepdims=True))
    goutq = mxq(f64(gout), 0, "e4m3")
    valsidxg = valsu[:, idx]
    c0 = goutq.T @ valsidxg
    dp = c0 / np.sum(p, axis=1, keepdims=True) + np.sum(c0 * p / np.square(np.sum(p, axis=1, keepdims=True)) * (-1.0), axis=1, keepdims=True)
    ds = dp * p
    dea = ds * f64(lam) / (ea + eb)
    tea = ta * np.exp(a) * f64(prior1)[:1][:, idx]
    ts = tea / (ea + eb) * f64(lam)
    tp = ts * p
    tdp = np.sum(tp, axis=1, keepdims=True) * c0 / np.square(np.sum(p, axis=1, keepdims=True)) * (-1.0) + np.sum((tp * c0 - np.sum(tp, axis=1, keepdims=True) * np.sum(p, axis=1, keepdims=True) * 2.0 * c0 * p / np.square(np.sum(p, axis=1, keepdims=True))) / np.square(np.sum(p, axis=1, keepdims=True)) * (-1.0), axis=1, keepdims=True)
    tds = tdp * p + tp * dp
    tdea = (tds * f64(lam) - tea * ds * f64(lam) / (ea + eb)) / (ea + eb)
    tda = tdea * f64(prior1)[:1][:, idx] * np.exp(a) + ta * np.exp(a) * dea * f64(prior1)[:1][:, idx]
    gs = tda * 512.0
    gf = np.zeros((Q, T))
    gf[:, idx] = gs
    y = f64(base) + gf
    return y

@@ -1,0 +1,201 @@
+from contextlib import ExitStack
+
+import concourse.mybir as mybir
+from concourse.masks import make_identity
+
+F32 = mybir.dt.float32
+BF16 = mybir.dt.bfloat16
+I32 = mybir.dt.int32
+U32 = mybir.dt.uint32
+U16 = mybir.dt.uint16
+U8 = mybir.dt.uint8
+FP8X4 = mybir.dt.float8_e4m3fn_x4
+ACT = mybir.ActivationFunctionType
+ALU = mybir.AluOpType
+
+P = 128
+PACK = 4
+T = 2048
+SLOTS = 512
+HALF = SLOTS // 2
+Q = 128
+LEAD = 128
+OUT_EDGES = (0, 512, 1024, 1536, 1792, 2048)
+
+FLOPS = 4 * 2 * 512 * Q * SLOTS
+BYTES = 6 * 2**20 + 2 * 16 * T + 4 * T + 4 * Q + 2 * SLOTS - 2**20
+
+
+def tile_attend_hveitherquestion_soft_s_kernel(
+    tc, query, query2, keys_words, keys_scales, prior1, lam, gout, vals_words, vals_scales, dquery, base, offs, out
+):
+    nc = tc.nc
+    with ExitStack() as ctx:
+        sb = ctx.enter_context(tc.tile_pool(name="sb", bufs=1))
+        ps = ctx.enter_context(tc.psum_pool(name="ps", bufs=1))
+
+        def wide(name):
+            return sb.tile([P, SLOTS], F32, name=name, tag=name, align_bytes=64)
+
+        def column(name):
+            return sb.tile([P, 1], F32, name=name)
+
+        offsets = sb.tile([P, SLOTS // 16], U16, name="offsets")
+        nc.sync.dma_start(offsets[:], offs)
+
+        def load_scales(name, scales, clear, queue, tag):
+            pool = sb.tile([P, T], U8, name=name, tag=tag, align_bytes=64)
+            clear.memset(pool[:].bitcast(I32), 0)
+            for r in range(4):
+                queue.dma_start(pool[r:P:32, :].bitcast(I32), scales[0][r:16:4, :].bitcast(I32))
+            return pool
+
+        def load_words(name, words, tag):
+            pool = sb.tile([P, T], U32, name=name, tag=tag, align_bytes=64)
+            nc.sync.dma_start(pool[:].bitcast(I32), words[0].rearrange("p n t -> p (n t)").bitcast(I32))
+            return pool
+
+        def load_rows(name, rows, tag):
+            raw = sb.tile([P, PACK, Q], F32, name=name, tag=tag, align_bytes=64)
+            nc.sync.dma_start(raw[:], rows.rearrange("(p j) q -> p j q", j=PACK))
+            return raw
+
+        def quantize(name, raw, cast):
+            grouped = sb.tile([P, Q, PACK], BF16, name=name + "_bf16", tag=name + "_bf16", align_bytes=64)
+            cast(grouped[:], raw[:].rearrange("p j q -> p q j"))
+            codes = sb.tile([P, Q], U32, name=name + "_codes", align_bytes=64)
+            scales = sb.tile([P, Q], U8, name=name + "_scales", align_bytes=64)
+            nc.vector.quantize_mx(out=codes[:].bitcast(FP8X4), scales=scales[:], in_=grouped[:].rearrange("p q j -> p (q j)"))
+            return codes, scales
+
+        def product(bank, rows, words, scales, cols):
+            nc.tensor.matmul_mx(
+                out=bank[:, cols], lhsT=rows[0][:].bitcast(FP8X4), lhsT_scale=rows[1][:],
+                rhs=words[:, cols].bitcast(FP8X4), rhs_scale=scales[:, cols], start=True, stop=True,
+            )
+
+        key_scale_pool = load_scales("key_scale_pool", keys_scales, nc.gpsimd, nc.scalar, "key_scale_pool")
+        lam_col = column("lam_col")
+        nc.gpsimd.dma_start(lam_col[:], lam)
+        query_raw = load_rows("query_raw", query, "query_raw")
+        prior_pool = sb.tile([P, T], F32, name="prior_pool", tag="prior_pool")
+        nc.vector.memset(prior_pool[:], 0.0)
+        nc.scalar.dma_start(prior_pool[0:1, :], prior1[0:1, :])
+        key_word_pool = load_words("key_word_pool", keys_words, "key_word_pool")
+        query2_raw = load_rows("query2_raw", query2, "query2_raw")
+        val_scale_pool = load_scales("val_scale_pool", vals_scales, nc.vector, nc.sync, "val_scale_pool")
+
+        neg_lam, lam_less_1 = column("neg_lam"), column("lam_less_1")
+        nc.scalar.activation(neg_lam[:], lam_col[:], ACT.Copy, scale=-1.0)
+        nc.scalar.activation(lam_less_1[:], lam_col[:], ACT.Identity, bias=-1.0)
+
+        identity = sb.tile([P, P], F32, name="identity")
+        make_identity(nc, identity[:])
+        placed = sb.tile([P, T], F32, name="placed")
+        nc.vector.memset(placed[:], 0.0)
+
+        key_scales = sb.tile([P, SLOTS], U8, name="key_scales", align_bytes=64)
+        nc.vector.tensor_copy(key_scales[:], key_scale_pool[:].indirect(offsets[:]))
+        query_mx = quantize("query", query_raw, nc.vector.tensor_copy)
+
+        prior_row = wide("prior_row")
+        for h in range(2):
+            nc.scalar.activation(
+                prior_row[:, h * HALF:(h + 1) * HALF], prior_pool[:].indirect(offsets[:, h * 16:(h + 1) * 16]), ACT.Copy
+            )
+        turned = ps.tile([P, 4, P], F32, name="turned")
+        for c in range(4):
+            nc.tensor.transpose(turned[:, c, :], prior_row[:, c * P:(c + 1) * P], identity[:])
+
+        key_words = sb.tile([P, SLOTS], U32, name="key_words", align_bytes=64)
+        a_bank = ps.tile([P, SLOTS], F32, name="a_bank")
+        for h in range(2):
+            cols = slice(h * HALF, (h + 1) * HALF)
+            nc.vector.tensor_copy(key_words[:, cols], key_word_pool[:].indirect(offsets[:, h * 16:(h + 1) * 16]))
+
+        prior_col = sb.tile([P, 4], F32, name="prior_col")
+        nc.vector.tensor_copy(prior_col[:], turned[:, :, 0])
+        query2_mx = quantize("query2", query2_raw, nc.scalar.copy)
+
+        dquery_raw = load_rows("dquery_raw", dquery, "query_bf16")
+        val_word_pool = load_words("val_word_pool", vals_words, "key_scale_pool")
+        gout_raw = load_rows("gout_raw", gout, "query2_raw")
+        base_sb = sb.tile([P, T], F32, name="base_sb", tag="prior_pool")
+        nc.sync.dma_start(base_sb[:], base)
+
+        for h in range(2):
+            product(a_bank, query_mx, key_words, key_scales, slice(h * HALF, (h + 1) * HALF))
+        b_bank = ps.tile([P, SLOTS], F32, name="b_bank")
+        product(b_bank, query2_mx, key_words, key_scales, slice(0, SLOTS))
+        prior_bank = ps.tile([P, SLOTS], F32, name="prior_bank")
+        for c in range(4):
+            nc.tensor.transpose(prior_bank[:, c * P:(c + 1) * P], prior_col[:, c:c + 1].to_broadcast([P, P]), identity[:])
+
+        exp_a, exp_b, ea, neg_eb, both = wide("exp_a"), wide("exp_b"), wide("ea"), wide("neg_eb"), wide("both")
+        nc.scalar.activation(exp_a[:], a_bank[:], ACT.Exp)
+        nc.scalar.activation(exp_b[:], b_bank[:], ACT.Exp)
+        nc.vector.tensor_tensor(ea[:], exp_a[:], prior_bank[:], ALU.mult)
+        nc.vector.scalar_tensor_tensor(neg_eb[:], prior_bank[:], 1.0, exp_b[:], ALU.subtract, ALU.mult)
+        nc.vector.tensor_tensor(both[:], ea[:], neg_eb[:], ALU.subtract)
+
+        ln_both, ln_ea = wide("ln_both"), wide("ln_ea")
+        lead, rest = slice(0, LEAD), slice(LEAD, SLOTS)
+        nc.scalar.activation(ln_ea[:], ea[:], ACT.Ln)
+        nc.scalar.activation(ln_both[:, lead], both[:, lead], ACT.Ln)
+        nc.scalar.activation(ln_both[:, rest], both[:, rest], ACT.Ln)
+
+        val_scales = sb.tile([P, SLOTS], U8, name="val_scales", align_bytes=64)
+        nc.vector.tensor_copy(val_scales[:], val_scale_pool[:].indirect(offsets[:]))
+        dquery_mx = quantize("dquery", dquery_raw, nc.vector.tensor_copy)
+        gout_mx = quantize("gout", gout_raw, nc.vector.tensor_copy)
+        val_words = sb.tile([P, SLOTS], U32, name="val_words", tag="neg_eb", align_bytes=64)
+        nc.vector.tensor_copy(val_words[:], val_word_pool[:].indirect(offsets[:]))
+        ta_bank = ps.tile([P, SLOTS], F32, name="ta_bank")
+        product(ta_bank, dquery_mx, key_words, key_scales, slice(0, SLOTS))
+        c0_bank = ps.tile([P, SLOTS], F32, name="c0_bank")
+        product(c0_bank, gout_mx, val_words, val_scales, slice(0, SLOTS))
+
+        neg_s, neg_max, ln_r, ln_rp = wide("neg_s"), column("neg_max"), wide("ln_r"), wide("ln_rp")
+        nc.vector.tensor_tensor(ln_r[:, lead], ln_ea[:, lead], ln_both[:, lead], ALU.subtract)
+        nc.vector.tensor_scalar(neg_s[:], ln_both[:], neg_lam[:], None, ALU.mult, ALU.min, accum_out=neg_max[:])
+        nc.vector.tensor_tensor(ln_r[:, rest], ln_ea[:, rest], ln_both[:, rest], ALU.subtract)
+        nc.vector.tensor_tensor(ln_rp[:], ln_r[:], neg_s[:], ALU.subtract)
+
+        p, p_sum, rp, r, curve = wide("p"), column("p_sum"), wide("rp"), wide("r"), wide("curve")
+        nc.scalar.activation(r[:, lead], ln_r[:, lead], ACT.Exp)
+        nc.scalar.activation(p[:], neg_s[:], ACT.Exp, scale=-1.0, bias=neg_max[:], accum_out=p_sum[:])
+        nc.scalar.activation(rp[:], ln_rp[:], ACT.Exp, bias=neg_max[:])
+        nc.scalar.activation(r[:, rest], ln_r[:, rest], ACT.Exp)
+        nc.scalar.activation(curve[:], r[:], ACT.Identity, scale=lam_less_1[:], bias=1.0)
+
+        inv_sum, neg_c_sum, neg_c_mean = column("inv_sum"), column("neg_c_sum"), column("neg_c_mean")
+        neg_pc, rpt, rpt_sum = wide("neg_pc"), wide("rpt"), column("rpt_sum")
+        nc.vector.scalar_tensor_tensor(neg_pc[:], c0_bank[:], -1.0, p[:], ALU.mult, ALU.mult, accum_out=neg_c_sum[:])
+        nc.vector.reciprocal(inv_sum[:], p_sum[:])
+        nc.vector.scalar_tensor_tensor(rpt[:], ta_bank[:], 1.0, rp[:], ALU.mult, ALU.mult, accum_out=rpt_sum[:])
+        nc.vector.tensor_tensor(neg_c_mean[:], neg_c_sum[:], inv_sum[:], ALU.mult)
+
+        lam_w, first, second = column("lam_w"), column("first"), column("second")
+        nc.gpsimd.tensor_scalar(lam_w[:], inv_sum[:], lam_col[:], 0.0, ALU.mult, ALU.add)
+        nc.gpsimd.tensor_scalar(first[:], lam_w[:], 512.0, 0.0, ALU.mult, ALU.add)
+        nc.gpsimd.tensor_scalar(second[:], first[:], lam_w[:], -1.0, ALU.mult, ALU.mult)
+
+        rptc, rptc_sum = wide("rptc"), column("rptc_sum")
+        nc.vector.scalar_tensor_tensor(rptc[:], c0_bank[:], neg_c_mean[:], rpt[:], ALU.add, ALU.mult, accum_out=rptc_sum[:])
+
+        slope, shift, mean_term = column("slope"), column("shift"), wide("mean_term")
+        nc.scalar.activation(slope[:], rpt_sum[:], ACT.Copy, scale=second[:])
+        nc.scalar.activation(shift[:], slope[:], ACT.Copy, scale=neg_c_mean[:])
+        nc.scalar.activation(mean_term[:], c0_bank[:], ACT.Identity, scale=slope[:], bias=shift[:])
+
+        cov_term, own, shared = column("cov_term"), wide("own"), wide("shared")
+        nc.vector.tensor_tensor(cov_term[:], rptc_sum[:], second[:], ALU.mult)
+        nc.vector.scalar_tensor_tensor(own[:], rptc[:], first[:], curve[:], ALU.mult, ALU.mult)
+        nc.vector.scalar_tensor_tensor(shared[:], mean_term[:], cov_term[:], rp[:], ALU.add, ALU.mult)
+        nc.vector.tensor_tensor(placed[:].indirect(offsets[:]), own[:], shared[:], ALU.add)
+
+        for c in range(len(OUT_EDGES) - 1):
+            cols = slice(OUT_EDGES[c], OUT_EDGES[c + 1])
+            result = sb.tile([P, cols.stop - cols.start], F32, name="result%d" % c)
+            nc.vector.tensor_tensor(result[:], placed[:, cols], base_sb[:, cols], ALU.add)
+            nc.sync.dma_start(out[:, cols], result[:])

@@ -19,7 +19,6 @@ T = 2048
 SLOTS = 512
 HALF = SLOTS // 2
 Q = 128
-LEAD = 128
 OUT_EDGES = (0, 512, 1024, 1536, 1792, 2048)
 
 FLOPS = 4 * 2 * 512 * Q * SLOTS
@@ -34,8 +33,8 @@ def tile_attend_hveitherquestion_soft_s_kernel(
         sb = ctx.enter_context(tc.tile_pool(name="sb", bufs=1))
         ps = ctx.enter_context(tc.psum_pool(name="ps", bufs=1))
 
-        def wide(name):
-            return sb.tile([P, SLOTS], F32, name=name, tag=name, align_bytes=64)
+        def wide(name, tag=None):
+            return sb.tile([P, SLOTS], F32, name=name, tag=tag or name, align_bytes=64)
 
         def column(name):
             return sb.tile([P, 1], F32, name=name)
@@ -50,122 +49,132 @@ def tile_attend_hveitherquestion_soft_s_kernel(
                 queue.dma_start(pool[r:P:32, :].bitcast(I32), scales[0][r:16:4, :].bitcast(I32))
             return pool
 
-        def load_words(name, words, tag):
+        def load_words(name, words, queue, tag):
             pool = sb.tile([P, T], U32, name=name, tag=tag, align_bytes=64)
-            nc.sync.dma_start(pool[:].bitcast(I32), words[0].rearrange("p n t -> p (n t)").bitcast(I32))
+            queue.dma_start(pool[:].bitcast(I32), words[0].rearrange("p n t -> p (n t)").bitcast(I32))
             return pool
 
-        def load_rows(name, rows, tag):
+        def load_rows(name, rows, queue, tag):
             raw = sb.tile([P, PACK, Q], F32, name=name, tag=tag, align_bytes=64)
-            nc.sync.dma_start(raw[:], rows.rearrange("(p j) q -> p j q", j=PACK))
+            queue.dma_start(raw[:], rows.rearrange("(p j) q -> p j q", j=PACK))
             return raw
 
-        def quantize(name, raw, cast):
-            grouped = sb.tile([P, Q, PACK], BF16, name=name + "_bf16", tag=name + "_bf16", align_bytes=64)
-            cast(grouped[:], raw[:].rearrange("p j q -> p q j"))
-            codes = sb.tile([P, Q], U32, name=name + "_codes", align_bytes=64)
-            scales = sb.tile([P, Q], U8, name=name + "_scales", align_bytes=64)
-            nc.vector.quantize_mx(out=codes[:].bitcast(FP8X4), scales=scales[:], in_=grouped[:].rearrange("p q j -> p (q j)"))
-            return codes, scales
+        def quantize_pair(name, raws, cast):
+            grouped = sb.tile([P, 2, Q, PACK], BF16, name=name + "_bf16", tag=name + "_bf16", align_bytes=64)
+            for k, raw in enumerate(raws):
+                cast(
+                    grouped[:, k].rearrange("p (c i) j -> p c j i", i=4), raw[:].rearrange("p j (c i) -> p c j i", i=4)
+                )
+            codes = sb.tile([P, 2 * Q], U32, name=name + "_codes", align_bytes=64)
+            scales = sb.tile([P, 2 * Q], U8, name=name + "_scales", align_bytes=64)
+            nc.vector.quantize_mx(
+                out=codes[:].bitcast(FP8X4), scales=scales[:], in_=grouped[:].rearrange("p k q j -> p (k q j)")
+            )
+            return [(codes[:, k * Q:(k + 1) * Q], scales[:, k * Q:(k + 1) * Q]) for k in range(2)]
 
-        def product(bank, rows, words, scales, cols):
+        def product(sums, rows, words, scales):
             nc.tensor.matmul_mx(
-                out=bank[:, cols], lhsT=rows[0][:].bitcast(FP8X4), lhsT_scale=rows[1][:],
-                rhs=words[:, cols].bitcast(FP8X4), rhs_scale=scales[:, cols], start=True, stop=True,
+                out=sums, lhsT=rows[0].bitcast(FP8X4), lhsT_scale=rows[1],
+                rhs=words.bitcast(FP8X4), rhs_scale=scales, start=True, stop=True,
             )
 
-        key_scale_pool = load_scales("key_scale_pool", keys_scales, nc.gpsimd, nc.scalar, "key_scale_pool")
-        lam_col = column("lam_col")
-        nc.gpsimd.dma_start(lam_col[:], lam)
-        query_raw = load_rows("query_raw", query, "query_raw")
+        key_scale_pool = load_scales("key_scale_pool", keys_scales, nc.gpsimd, nc.sync, "key_scale_pool")
+        query_raw = load_rows("query_raw", query, nc.scalar, "query_raw")
         prior_pool = sb.tile([P, T], F32, name="prior_pool", tag="prior_pool")
         nc.vector.memset(prior_pool[:], 0.0)
-        nc.scalar.dma_start(prior_pool[0:1, :], prior1[0:1, :])
-        key_word_pool = load_words("key_word_pool", keys_words, "key_word_pool")
-        query2_raw = load_rows("query2_raw", query2, "query2_raw")
-        val_scale_pool = load_scales("val_scale_pool", vals_scales, nc.vector, nc.sync, "val_scale_pool")
-
-        neg_lam, lam_less_1 = column("neg_lam"), column("lam_less_1")
-        nc.scalar.activation(neg_lam[:], lam_col[:], ACT.Copy, scale=-1.0)
-        nc.scalar.activation(lam_less_1[:], lam_col[:], ACT.Identity, bias=-1.0)
+        nc.sync.dma_start(prior_pool[0:1, :], prior1[0:1, :])
+        query2_raw = load_rows("query2_raw", query2, nc.scalar, "query2_raw")
+        key_word_pool = load_words("key_word_pool", keys_words, nc.scalar, "key_word_pool")
 
         identity = sb.tile([P, P], F32, name="identity")
         make_identity(nc, identity[:])
+        lam_col = column("lam_col")
+        nc.gpsimd.dma_start(lam_col[:], lam)
+        neg_lam, lam_less_1 = column("neg_lam"), column("lam_less_1")
+        nc.gpsimd.tensor_scalar(neg_lam[:], lam_col[:], -1.0, 0.0, ALU.mult, ALU.add)
+        nc.gpsimd.tensor_scalar(lam_less_1[:], lam_col[:], 1.0, -1.0, ALU.mult, ALU.add)
+        lam_512, neg_lam2_512 = column("lam_512"), column("neg_lam2_512")
+        nc.gpsimd.tensor_scalar(lam_512[:], lam_col[:], 512.0, 0.0, ALU.mult, ALU.add)
+        nc.gpsimd.tensor_scalar(neg_lam2_512[:], lam_col[:], lam_col[:], -512.0, ALU.mult, ALU.mult)
         placed = sb.tile([P, T], F32, name="placed")
-        nc.vector.memset(placed[:], 0.0)
 
         key_scales = sb.tile([P, SLOTS], U8, name="key_scales", align_bytes=64)
         nc.vector.tensor_copy(key_scales[:], key_scale_pool[:].indirect(offsets[:]))
-        query_mx = quantize("query", query_raw, nc.vector.tensor_copy)
+        query_mx, query2_mx = quantize_pair("questions", (query_raw, query2_raw), nc.scalar.copy)
+
+        halves = [slice(h * HALF, (h + 1) * HALF) for h in range(2)]
+        half_offsets = [offsets[:, h * 16:(h + 1) * 16] for h in range(2)]
 
         prior_row = wide("prior_row")
         for h in range(2):
-            nc.scalar.activation(
-                prior_row[:, h * HALF:(h + 1) * HALF], prior_pool[:].indirect(offsets[:, h * 16:(h + 1) * 16]), ACT.Copy
-            )
-        turned = ps.tile([P, 4, P], F32, name="turned")
-        for c in range(4):
-            nc.tensor.transpose(turned[:, c, :], prior_row[:, c * P:(c + 1) * P], identity[:])
+            nc.scalar.activation(prior_row[:, halves[h]], prior_pool[:].indirect(half_offsets[h]), ACT.Copy)
+        prior_banks = []
+        for h in range(2):
+            turned = ps.tile([P, 2, P], F32, name="turned%d" % h)
+            for c in range(2):
+                nc.tensor.transpose(turned[:, c, :], prior_row[:, h * HALF + c * P:h * HALF + (c + 1) * P], identity[:])
+            prior_col = sb.tile([P, 2], F32, name="prior_col%d" % h)
+            nc.vector.tensor_copy(prior_col[:], turned[:, :, 0])
+            bank = ps.tile([P, HALF], F32, name="prior_bank%d" % h)
+            for c in range(2):
+                nc.tensor.transpose(bank[:, c * P:(c + 1) * P], prior_col[:, c:c + 1].to_broadcast([P, P]), identity[:])
+            prior_banks.append(bank)
 
         key_words = sb.tile([P, SLOTS], U32, name="key_words", align_bytes=64)
-        a_bank = ps.tile([P, SLOTS], F32, name="a_bank")
         for h in range(2):
-            cols = slice(h * HALF, (h + 1) * HALF)
-            nc.vector.tensor_copy(key_words[:, cols], key_word_pool[:].indirect(offsets[:, h * 16:(h + 1) * 16]))
+            nc.vector.tensor_copy(key_words[:, halves[h]], key_word_pool[:].indirect(half_offsets[h]))
 
-        prior_col = sb.tile([P, 4], F32, name="prior_col")
-        nc.vector.tensor_copy(prior_col[:], turned[:, :, 0])
-        query2_mx = quantize("query2", query2_raw, nc.scalar.copy)
+        for c in range(4):
+            nc.vector.memset(placed[:, c * 512:(c + 1) * 512], 0.0)
 
-        dquery_raw = load_rows("dquery_raw", dquery, "query_bf16")
-        val_word_pool = load_words("val_word_pool", vals_words, "key_scale_pool")
-        gout_raw = load_rows("gout_raw", gout, "query2_raw")
+        val_scale_pool = load_scales("val_scale_pool", vals_scales, nc.vector, nc.sync, "val_scale_pool")
+        val_word_pool = load_words("val_word_pool", vals_words, nc.sync, "key_scale_pool")
+        dquery_raw = load_rows("dquery_raw", dquery, nc.sync, "query_raw")
+        gout_raw = load_rows("gout_raw", gout, nc.sync, "query2_raw")
         base_sb = sb.tile([P, T], F32, name="base_sb", tag="prior_pool")
         nc.sync.dma_start(base_sb[:], base)
 
-        for h in range(2):
-            product(a_bank, query_mx, key_words, key_scales, slice(h * HALF, (h + 1) * HALF))
-        b_bank = ps.tile([P, SLOTS], F32, name="b_bank")
-        product(b_bank, query2_mx, key_words, key_scales, slice(0, SLOTS))
-        prior_bank = ps.tile([P, SLOTS], F32, name="prior_bank")
-        for c in range(4):
-            nc.tensor.transpose(prior_bank[:, c * P:(c + 1) * P], prior_col[:, c:c + 1].to_broadcast([P, P]), identity[:])
+        dquery_mx, gout_mx = quantize_pair("directions", (dquery_raw, gout_raw), nc.vector.tensor_copy)
+        val_scales = sb.tile([P, SLOTS], U8, name="val_scales", align_bytes=64)
+        nc.vector.tensor_copy(val_scales[:], val_scale_pool[:].indirect(offsets[:]))
 
-        exp_a, exp_b, ea, neg_eb, both = wide("exp_a"), wide("exp_b"), wide("ea"), wide("neg_eb"), wide("both")
-        nc.scalar.activation(exp_a[:], a_bank[:], ACT.Exp)
-        nc.scalar.activation(exp_b[:], b_bank[:], ACT.Exp)
-        nc.vector.tensor_tensor(ea[:], exp_a[:], prior_bank[:], ALU.mult)
-        nc.vector.scalar_tensor_tensor(neg_eb[:], prior_bank[:], 1.0, exp_b[:], ALU.subtract, ALU.mult)
+        ea, neg_eb, both = wide("ea"), wide("neg_eb", "val_scale_pool"), wide("both", "directions_bf16")
+        exps = []
+        for h in range(2):
+            ab_bank = ps.tile([P, 2, HALF], F32, name="ab_bank%d" % h)
+            product(ab_bank[:, 0, :], query_mx, key_words[:, halves[h]], key_scales[:, halves[h]])
+            product(ab_bank[:, 1, :], query2_mx, key_words[:, halves[h]], key_scales[:, halves[h]])
+            exp_ab = sb.tile([P, 2, HALF], F32, name="exp_ab%d" % h)
+            nc.scalar.activation(exp_ab[:], ab_bank[:], ACT.Exp)
+            exps.append(exp_ab)
+        for h in range(2):
+            nc.vector.tensor_tensor(ea[:, halves[h]], exps[h][:, 0, :], prior_banks[h][:], ALU.mult)
+            nc.vector.scalar_tensor_tensor(
+                neg_eb[:, halves[h]], prior_banks[h][:], 1.0, exps[h][:, 1, :], ALU.subtract, ALU.mult
+            )
         nc.vector.tensor_tensor(both[:], ea[:], neg_eb[:], ALU.subtract)
 
         ln_both, ln_ea = wide("ln_both"), wide("ln_ea")
-        lead, rest = slice(0, LEAD), slice(LEAD, SLOTS)
         nc.scalar.activation(ln_ea[:], ea[:], ACT.Ln)
-        nc.scalar.activation(ln_both[:, lead], both[:, lead], ACT.Ln)
-        nc.scalar.activation(ln_both[:, rest], both[:, rest], ACT.Ln)
+        nc.scalar.activation(ln_both[:], both[:], ACT.Ln)
 
-        val_scales = sb.tile([P, SLOTS], U8, name="val_scales", align_bytes=64)
-        nc.vector.tensor_copy(val_scales[:], val_scale_pool[:].indirect(offsets[:]))
-        dquery_mx = quantize("dquery", dquery_raw, nc.vector.tensor_copy)
-        gout_mx = quantize("gout", gout_raw, nc.vector.tensor_copy)
-        val_words = sb.tile([P, SLOTS], U32, name="val_words", tag="neg_eb", align_bytes=64)
+        val_words = sb.tile([P, SLOTS], U32, name="val_words", tag="val_scale_pool", align_bytes=64)
         nc.vector.tensor_copy(val_words[:], val_word_pool[:].indirect(offsets[:]))
         ta_bank = ps.tile([P, SLOTS], F32, name="ta_bank")
-        product(ta_bank, dquery_mx, key_words, key_scales, slice(0, SLOTS))
+        product(ta_bank[:], dquery_mx, key_words[:], key_scales[:])
         c0_bank = ps.tile([P, SLOTS], F32, name="c0_bank")
-        product(c0_bank, gout_mx, val_words, val_scales, slice(0, SLOTS))
+        product(c0_bank[:], gout_mx, val_words[:], val_scales[:])
 
-        neg_s, neg_max, ln_r, ln_rp = wide("neg_s"), column("neg_max"), wide("ln_r"), wide("ln_rp")
-        nc.vector.tensor_tensor(ln_r[:, lead], ln_ea[:, lead], ln_both[:, lead], ALU.subtract)
+        neg_s = wide("neg_s", "key_scale_pool")
+        neg_max, ln_r, ln_rp = column("neg_max"), wide("ln_r"), wide("ln_rp")
         nc.vector.tensor_scalar(neg_s[:], ln_both[:], neg_lam[:], None, ALU.mult, ALU.min, accum_out=neg_max[:])
-        nc.vector.tensor_tensor(ln_r[:, rest], ln_ea[:, rest], ln_both[:, rest], ALU.subtract)
-        nc.vector.tensor_tensor(ln_rp[:], ln_r[:], neg_s[:], ALU.subtract)
+        nc.vector.scalar_tensor_tensor(ln_rp[:], ln_both[:], lam_less_1[:], ln_ea[:], ALU.mult, ALU.add)
+        nc.vector.tensor_tensor(ln_r[:], ln_ea[:], ln_both[:], ALU.subtract)
 
         p, p_sum, rp, r, curve = wide("p"), column("p_sum"), wide("rp"), wide("r"), wide("curve")
-        nc.scalar.activation(r[:, lead], ln_r[:, lead], ACT.Exp)
         nc.scalar.activation(p[:], neg_s[:], ACT.Exp, scale=-1.0, bias=neg_max[:], accum_out=p_sum[:])
         nc.scalar.activation(rp[:], ln_rp[:], ACT.Exp, bias=neg_max[:])
-        nc.scalar.activation(r[:, rest], ln_r[:, rest], ACT.Exp)
+        nc.scalar.activation(r[:], ln_r[:], ACT.Exp)
         nc.scalar.activation(curve[:], r[:], ACT.Identity, scale=lam_less_1[:], bias=1.0)
 
         inv_sum, neg_c_sum, neg_c_mean = column("inv_sum"), column("neg_c_sum"), column("neg_c_mean")
@@ -175,17 +184,16 @@ def tile_attend_hveitherquestion_soft_s_kernel(
         nc.vector.scalar_tensor_tensor(rpt[:], ta_bank[:], 1.0, rp[:], ALU.mult, ALU.mult, accum_out=rpt_sum[:])
         nc.vector.tensor_tensor(neg_c_mean[:], neg_c_sum[:], inv_sum[:], ALU.mult)
 
-        lam_w, first, second = column("lam_w"), column("first"), column("second")
-        nc.gpsimd.tensor_scalar(lam_w[:], inv_sum[:], lam_col[:], 0.0, ALU.mult, ALU.add)
-        nc.gpsimd.tensor_scalar(first[:], lam_w[:], 512.0, 0.0, ALU.mult, ALU.add)
-        nc.gpsimd.tensor_scalar(second[:], first[:], lam_w[:], -1.0, ALU.mult, ALU.mult)
+        first, second, slope, shift = column("first"), column("second"), column("slope"), column("shift")
+        nc.gpsimd.tensor_scalar(second[:], inv_sum[:], inv_sum[:], neg_lam2_512[:], ALU.mult, ALU.mult)
+        nc.gpsimd.tensor_scalar(first[:], inv_sum[:], lam_512[:], 0.0, ALU.mult, ALU.add)
+        nc.gpsimd.tensor_scalar(slope[:], rpt_sum[:], second[:], 0.0, ALU.mult, ALU.add)
+        nc.gpsimd.tensor_scalar(shift[:], rpt_sum[:], second[:], neg_c_mean[:], ALU.mult, ALU.mult)
 
         rptc, rptc_sum = wide("rptc"), column("rptc_sum")
         nc.vector.scalar_tensor_tensor(rptc[:], c0_bank[:], neg_c_mean[:], rpt[:], ALU.add, ALU.mult, accum_out=rptc_sum[:])
 
-        slope, shift, mean_term = column("slope"), column("shift"), wide("mean_term")
-        nc.scalar.activation(slope[:], rpt_sum[:], ACT.Copy, scale=second[:])
-        nc.scalar.activation(shift[:], slope[:], ACT.Copy, scale=neg_c_mean[:])
+        mean_term = wide("mean_term")
         nc.scalar.activation(mean_term[:], c0_bank[:], ACT.Identity, scale=slope[:], bias=shift[:])
 
         cov_term, own, shared = column("cov_term"), wide("own"), wide("shared")

@@ -42,11 +42,11 @@ def tile_attend_hveitherquestion_soft_s_kernel(
         offsets = sb.tile([P, SLOTS // 16], U16, name="offsets")
         nc.sync.dma_start(offsets[:], offs)
 
-        def load_scales(name, scales, clear, queue, tag):
+        def load_scales(name, scales, clear, queues, tag):
             pool = sb.tile([P, T], U8, name=name, tag=tag, align_bytes=64)
             clear.memset(pool[:].bitcast(I32), 0)
             for r in range(4):
-                queue.dma_start(pool[r:P:32, :].bitcast(I32), scales[0][r:16:4, :].bitcast(I32))
+                queues[r % 2].dma_start(pool[r:P:32, :].bitcast(I32), scales[0][r:16:4, :].bitcast(I32))
             return pool
 
         def load_words(name, words, queue, tag):
@@ -63,7 +63,7 @@ def tile_attend_hveitherquestion_soft_s_kernel(
             grouped = sb.tile([P, 2, Q, PACK], BF16, name=name + "_bf16", tag=name + "_bf16", align_bytes=64)
             for k, raw in enumerate(raws):
                 cast(
-                    grouped[:, k].rearrange("p (c i) j -> p c j i", i=4), raw[:].rearrange("p j (c i) -> p c j i", i=4)
+                    grouped[:, k].rearrange("p (c i) j -> p c j i", i=4), raw.rearrange("p j (c i) -> p c j i", i=4)
                 )
             codes = sb.tile([P, 2 * Q], U32, name=name + "_codes", align_bytes=64)
             scales = sb.tile([P, 2 * Q], U8, name=name + "_scales", align_bytes=64)
@@ -78,87 +78,83 @@ def tile_attend_hveitherquestion_soft_s_kernel(
                 rhs=words.bitcast(FP8X4), rhs_scale=scales, start=True, stop=True,
             )
 
-        key_scale_pool = load_scales("key_scale_pool", keys_scales, nc.gpsimd, nc.sync, "key_scale_pool")
-        query_raw = load_rows("query_raw", query, nc.scalar, "query_raw")
+        key_scale_pool = load_scales("key_scale_pool", keys_scales, nc.gpsimd, (nc.sync, nc.scalar), "key_scale_pool")
+        lam_col = column("lam_col")
+        nc.gpsimd.dma_start(lam_col[:], lam)
+        query_raw = load_rows("query_raw", query, nc.sync, "query_raw")
         prior_pool = sb.tile([P, T], F32, name="prior_pool", tag="prior_pool")
         nc.vector.memset(prior_pool[:], 0.0)
-        nc.sync.dma_start(prior_pool[0:1, :], prior1[0:1, :])
-        query2_raw = load_rows("query2_raw", query2, nc.scalar, "query2_raw")
-        key_word_pool = load_words("key_word_pool", keys_words, nc.scalar, "key_word_pool")
+        nc.scalar.dma_start(prior_pool[0:1, :], prior1[0:1, :])
+        query2_raw = load_rows("query2_raw", query2, nc.sync, "query2_raw")
+        key_word_pool = load_words("key_word_pool", keys_words, nc.sync, "key_word_pool")
 
         identity = sb.tile([P, P], F32, name="identity")
         make_identity(nc, identity[:])
-        lam_col = column("lam_col")
-        nc.gpsimd.dma_start(lam_col[:], lam)
         neg_lam, lam_less_1 = column("neg_lam"), column("lam_less_1")
-        nc.gpsimd.tensor_scalar(neg_lam[:], lam_col[:], -1.0, 0.0, ALU.mult, ALU.add)
+        nc.scalar.activation(neg_lam[:], lam_col[:], ACT.Copy, scale=-1.0)
         nc.gpsimd.tensor_scalar(lam_less_1[:], lam_col[:], 1.0, -1.0, ALU.mult, ALU.add)
         lam_512, neg_lam2_512 = column("lam_512"), column("neg_lam2_512")
         nc.gpsimd.tensor_scalar(lam_512[:], lam_col[:], 512.0, 0.0, ALU.mult, ALU.add)
         nc.gpsimd.tensor_scalar(neg_lam2_512[:], lam_col[:], lam_col[:], -512.0, ALU.mult, ALU.mult)
-        placed = sb.tile([P, T], F32, name="placed")
 
-        key_scales = sb.tile([P, SLOTS], U8, name="key_scales", align_bytes=64)
+        query_mx, query2_mx = quantize_pair("questions", (query_raw[:], query2_raw[:]), nc.vector.tensor_copy)
+        directions_raw = sb.tile([P, 2, PACK, Q], F32, name="directions_raw", tag="query_raw", align_bytes=64)
+        for k, rows in enumerate((dquery, gout)):
+            nc.sync.dma_start(directions_raw[:, k], rows.rearrange("(p j) q -> p j q", j=PACK))
+        val_scale_pool = load_scales("val_scale_pool", vals_scales, nc.vector, (nc.sync, nc.sync), "query2_raw")
+        key_scales = sb.tile([P, SLOTS], U8, name="key_scales", tag="questions_bf16", align_bytes=64)
         nc.vector.tensor_copy(key_scales[:], key_scale_pool[:].indirect(offsets[:]))
-        query_mx, query2_mx = quantize_pair("questions", (query_raw, query2_raw), nc.scalar.copy)
 
         halves = [slice(h * HALF, (h + 1) * HALF) for h in range(2)]
         half_offsets = [offsets[:, h * 16:(h + 1) * 16] for h in range(2)]
-
-        prior_row = wide("prior_row")
-        for h in range(2):
-            nc.scalar.activation(prior_row[:, halves[h]], prior_pool[:].indirect(half_offsets[h]), ACT.Copy)
-        prior_banks = []
-        for h in range(2):
-            turned = ps.tile([P, 2, P], F32, name="turned%d" % h)
-            for c in range(2):
-                nc.tensor.transpose(turned[:, c, :], prior_row[:, h * HALF + c * P:h * HALF + (c + 1) * P], identity[:])
-            prior_col = sb.tile([P, 2], F32, name="prior_col%d" % h)
-            nc.vector.tensor_copy(prior_col[:], turned[:, :, 0])
-            bank = ps.tile([P, HALF], F32, name="prior_bank%d" % h)
-            for c in range(2):
-                nc.tensor.transpose(bank[:, c * P:(c + 1) * P], prior_col[:, c:c + 1].to_broadcast([P, P]), identity[:])
-            prior_banks.append(bank)
 
         key_words = sb.tile([P, SLOTS], U32, name="key_words", align_bytes=64)
         for h in range(2):
             nc.vector.tensor_copy(key_words[:, halves[h]], key_word_pool[:].indirect(half_offsets[h]))
 
+        prior_row = wide("prior_row")
+        for h in range(2):
+            nc.scalar.activation(prior_row[:, halves[h]], prior_pool[:].indirect(half_offsets[h]), ACT.Copy)
+        turned = ps.tile([P, 4, P], F32, name="turned")
         for c in range(4):
-            nc.vector.memset(placed[:, c * 512:(c + 1) * 512], 0.0)
+            nc.tensor.transpose(turned[:, c, :], prior_row[:, c * P:(c + 1) * P], identity[:])
+        prior_col = sb.tile([P, 4], F32, name="prior_col", tag="key_word_pool", align_bytes=64)
+        nc.vector.tensor_copy(prior_col[:], turned[:, :, 0])
+        prior_bank = ps.tile([P, 2, HALF], F32, name="prior_bank")
+        for c in range(4):
+            nc.tensor.transpose(
+                prior_bank[:, c // 2, (c % 2) * P:(c % 2 + 1) * P], prior_col[:, c:c + 1].to_broadcast([P, P]), identity[:]
+            )
 
-        val_scale_pool = load_scales("val_scale_pool", vals_scales, nc.vector, nc.sync, "val_scale_pool")
         val_word_pool = load_words("val_word_pool", vals_words, nc.sync, "key_scale_pool")
-        dquery_raw = load_rows("dquery_raw", dquery, nc.sync, "query_raw")
-        gout_raw = load_rows("gout_raw", gout, nc.sync, "query2_raw")
         base_sb = sb.tile([P, T], F32, name="base_sb", tag="prior_pool")
         nc.sync.dma_start(base_sb[:], base)
 
-        dquery_mx, gout_mx = quantize_pair("directions", (dquery_raw, gout_raw), nc.vector.tensor_copy)
+        dquery_mx, gout_mx = quantize_pair("directions", (directions_raw[:, 0], directions_raw[:, 1]), nc.vector.tensor_copy)
         val_scales = sb.tile([P, SLOTS], U8, name="val_scales", align_bytes=64)
         nc.vector.tensor_copy(val_scales[:], val_scale_pool[:].indirect(offsets[:]))
 
-        ea, neg_eb, both = wide("ea"), wide("neg_eb", "val_scale_pool"), wide("both", "directions_bf16")
-        exps = []
+        ea, neg_eb, both = wide("ea"), wide("neg_eb", "query2_raw"), wide("both", "directions_bf16")
+        exp_ab = sb.tile([P, 2, 2, HALF], F32, name="exp_ab", align_bytes=64)
         for h in range(2):
             ab_bank = ps.tile([P, 2, HALF], F32, name="ab_bank%d" % h)
             product(ab_bank[:, 0, :], query_mx, key_words[:, halves[h]], key_scales[:, halves[h]])
             product(ab_bank[:, 1, :], query2_mx, key_words[:, halves[h]], key_scales[:, halves[h]])
-            exp_ab = sb.tile([P, 2, HALF], F32, name="exp_ab%d" % h)
-            nc.scalar.activation(exp_ab[:], ab_bank[:], ACT.Exp)
-            exps.append(exp_ab)
-        for h in range(2):
-            nc.vector.tensor_tensor(ea[:, halves[h]], exps[h][:, 0, :], prior_banks[h][:], ALU.mult)
-            nc.vector.scalar_tensor_tensor(
-                neg_eb[:, halves[h]], prior_banks[h][:], 1.0, exps[h][:, 1, :], ALU.subtract, ALU.mult
-            )
+            nc.scalar.activation(exp_ab[:, :, h, :], ab_bank[:], ACT.Exp)
+        flat_prior = prior_bank[:].rearrange("p h i -> p (h i)")
+        nc.vector.tensor_tensor(ea[:], exp_ab[:, 0].rearrange("p h i -> p (h i)"), flat_prior, ALU.mult)
+        nc.vector.scalar_tensor_tensor(
+            neg_eb[:], flat_prior, 1.0, exp_ab[:, 1].rearrange("p h i -> p (h i)"), ALU.subtract, ALU.mult
+        )
         nc.vector.tensor_tensor(both[:], ea[:], neg_eb[:], ALU.subtract)
 
         ln_both, ln_ea = wide("ln_both"), wide("ln_ea")
         nc.scalar.activation(ln_ea[:], ea[:], ACT.Ln)
         nc.scalar.activation(ln_both[:], both[:], ACT.Ln)
+        placed = sb.tile([P, T], F32, name="placed", tag="ea", align_bytes=64)
+        nc.gpsimd.memset(placed[:], 0.0)
 
-        val_words = sb.tile([P, SLOTS], U32, name="val_words", tag="val_scale_pool", align_bytes=64)
+        val_words = sb.tile([P, SLOTS], U32, name="val_words", tag="query2_raw", align_bytes=64)
         nc.vector.tensor_copy(val_words[:], val_word_pool[:].indirect(offsets[:]))
         ta_bank = ps.tile([P, SLOTS], F32, name="ta_bank")
         product(ta_bank[:], dquery_mx, key_words[:], key_scales[:])
@@ -179,10 +175,10 @@ def tile_attend_hveitherquestion_soft_s_kernel(
 
         inv_sum, neg_c_sum, neg_c_mean = column("inv_sum"), column("neg_c_sum"), column("neg_c_mean")
         neg_pc, rpt, rpt_sum = wide("neg_pc"), wide("rpt"), column("rpt_sum")
-        nc.vector.scalar_tensor_tensor(neg_pc[:], c0_bank[:], -1.0, p[:], ALU.mult, ALU.mult, accum_out=neg_c_sum[:])
         nc.vector.reciprocal(inv_sum[:], p_sum[:])
+        nc.vector.scalar_tensor_tensor(neg_pc[:], c0_bank[:], -1.0, p[:], ALU.mult, ALU.mult, accum_out=neg_c_sum[:])
         nc.vector.scalar_tensor_tensor(rpt[:], ta_bank[:], 1.0, rp[:], ALU.mult, ALU.mult, accum_out=rpt_sum[:])
-        nc.vector.tensor_tensor(neg_c_mean[:], neg_c_sum[:], inv_sum[:], ALU.mult)
+        nc.gpsimd.tensor_scalar(neg_c_mean[:], neg_c_sum[:], inv_sum[:], 0.0, ALU.mult, ALU.add)
 
         first, second, slope, shift = column("first"), column("second"), column("slope"), column("shift")
         nc.gpsimd.tensor_scalar(second[:], inv_sum[:], inv_sum[:], neg_lam2_512[:], ALU.mult, ALU.mult)

from contextlib import ExitStack

import concourse.mybir as mybir
from concourse.masks import make_identity

F32 = mybir.dt.float32
BF16 = mybir.dt.bfloat16
I32 = mybir.dt.int32
U32 = mybir.dt.uint32
U16 = mybir.dt.uint16
U8 = mybir.dt.uint8
FP8X4 = mybir.dt.float8_e4m3fn_x4
ACT = mybir.ActivationFunctionType
ALU = mybir.AluOpType

P = 128
PACK = 4
T = 2048
SLOTS = 512
HALF = SLOTS // 2
Q = 128
OUT_EDGES = (0, 512, 1024, 1536, 1792, 2048)

FLOPS = 4 * 2 * 512 * Q * SLOTS
BYTES = 6 * 2**20 + 2 * 16 * T + 4 * T + 4 * Q + 2 * SLOTS - 2**20


def tile_attend_hveitherquestion_soft_s_kernel(
    tc, query, query2, keys_words, keys_scales, prior1, lam, gout, vals_words, vals_scales, dquery, base, offs, out
):
    nc = tc.nc
    with ExitStack() as ctx:
        sb = ctx.enter_context(tc.tile_pool(name="sb", bufs=1))
        ps = ctx.enter_context(tc.psum_pool(name="ps", bufs=1))

        def wide(name, tag=None):
            return sb.tile([P, SLOTS], F32, name=name, tag=tag or name, align_bytes=64)

        def column(name):
            return sb.tile([P, 1], F32, name=name)

        offsets = sb.tile([P, SLOTS // 16], U16, name="offsets")
        nc.sync.dma_start(offsets[:], offs)

        def load_scales(name, scales, clear, queues, tag):
            pool = sb.tile([P, T], U8, name=name, tag=tag, align_bytes=64)
            clear.memset(pool[:].bitcast(I32), 0)
            for r in range(4):
                queues[r % 2].dma_start(pool[r:P:32, :].bitcast(I32), scales[0][r:16:4, :].bitcast(I32))
            return pool

        def load_words(name, words, queue, tag):
            pool = sb.tile([P, T], U32, name=name, tag=tag, align_bytes=64)
            queue.dma_start(pool[:].bitcast(I32), words[0].rearrange("p n t -> p (n t)").bitcast(I32))
            return pool

        def load_rows(name, rows, queue, tag):
            raw = sb.tile([P, PACK, Q], F32, name=name, tag=tag, align_bytes=64)
            queue.dma_start(raw[:], rows.rearrange("(p j) q -> p j q", j=PACK))
            return raw

        def quantize_pair(name, raws, cast):
            grouped = sb.tile([P, 2, Q, PACK], BF16, name=name + "_bf16", tag=name + "_bf16", align_bytes=64)
            for k, raw in enumerate(raws):
                cast(
                    grouped[:, k].rearrange("p (c i) j -> p c j i", i=4), raw.rearrange("p j (c i) -> p c j i", i=4)
                )
            codes = sb.tile([P, 2 * Q], U32, name=name + "_codes", align_bytes=64)
            scales = sb.tile([P, 2 * Q], U8, name=name + "_scales", align_bytes=64)
            nc.vector.quantize_mx(
                out=codes[:].bitcast(FP8X4), scales=scales[:], in_=grouped[:].rearrange("p k q j -> p (k q j)")
            )
            return [(codes[:, k * Q:(k + 1) * Q], scales[:, k * Q:(k + 1) * Q]) for k in range(2)]

        def product(sums, rows, words, scales):
            nc.tensor.matmul_mx(
                out=sums, lhsT=rows[0].bitcast(FP8X4), lhsT_scale=rows[1],
                rhs=words.bitcast(FP8X4), rhs_scale=scales, start=True, stop=True,
            )

        key_scale_pool = load_scales("key_scale_pool", keys_scales, nc.gpsimd, (nc.sync, nc.scalar), "key_scale_pool")
        lam_col = column("lam_col")
        nc.gpsimd.dma_start(lam_col[:], lam)
        query_raw = load_rows("query_raw", query, nc.sync, "query_raw")
        prior_pool = sb.tile([P, T], F32, name="prior_pool", tag="prior_pool")
        nc.vector.memset(prior_pool[:], 0.0)
        nc.scalar.dma_start(prior_pool[0:1, :], prior1[0:1, :])
        query2_raw = load_rows("query2_raw", query2, nc.sync, "query2_raw")
        key_word_pool = load_words("key_word_pool", keys_words, nc.sync, "key_word_pool")

        identity = sb.tile([P, P], F32, name="identity")
        make_identity(nc, identity[:])
        neg_lam, lam_less_1 = column("neg_lam"), column("lam_less_1")
        nc.scalar.activation(neg_lam[:], lam_col[:], ACT.Copy, scale=-1.0)
        nc.gpsimd.tensor_scalar(lam_less_1[:], lam_col[:], 1.0, -1.0, ALU.mult, ALU.add)
        lam_512, neg_lam2_512 = column("lam_512"), column("neg_lam2_512")
        nc.gpsimd.tensor_scalar(lam_512[:], lam_col[:], 512.0, 0.0, ALU.mult, ALU.add)
        nc.gpsimd.tensor_scalar(neg_lam2_512[:], lam_col[:], lam_col[:], -512.0, ALU.mult, ALU.mult)

        query_mx, query2_mx = quantize_pair("questions", (query_raw[:], query2_raw[:]), nc.vector.tensor_copy)
        directions_raw = sb.tile([P, 2, PACK, Q], F32, name="directions_raw", tag="query_raw", align_bytes=64)
        for k, rows in enumerate((dquery, gout)):
            nc.sync.dma_start(directions_raw[:, k], rows.rearrange("(p j) q -> p j q", j=PACK))
        val_scale_pool = load_scales("val_scale_pool", vals_scales, nc.vector, (nc.sync, nc.sync), "query2_raw")
        key_scales = sb.tile([P, SLOTS], U8, name="key_scales", tag="questions_bf16", align_bytes=64)
        nc.vector.tensor_copy(key_scales[:], key_scale_pool[:].indirect(offsets[:]))

        halves = [slice(h * HALF, (h + 1) * HALF) for h in range(2)]
        half_offsets = [offsets[:, h * 16:(h + 1) * 16] for h in range(2)]

        key_words = sb.tile([P, SLOTS], U32, name="key_words", align_bytes=64)
        for h in range(2):
            nc.vector.tensor_copy(key_words[:, halves[h]], key_word_pool[:].indirect(half_offsets[h]))

        prior_row = wide("prior_row")
        for h in range(2):
            nc.scalar.activation(prior_row[:, halves[h]], prior_pool[:].indirect(half_offsets[h]), ACT.Copy)
        turned = ps.tile([P, 4, P], F32, name="turned")
        for c in range(4):
            nc.tensor.transpose(turned[:, c, :], prior_row[:, c * P:(c + 1) * P], identity[:])
        prior_col = sb.tile([P, 4], F32, name="prior_col", tag="key_word_pool", align_bytes=64)
        nc.vector.tensor_copy(prior_col[:], turned[:, :, 0])
        prior_bank = ps.tile([P, 2, HALF], F32, name="prior_bank")
        for c in range(4):
            nc.tensor.transpose(
                prior_bank[:, c // 2, (c % 2) * P:(c % 2 + 1) * P], prior_col[:, c:c + 1].to_broadcast([P, P]), identity[:]
            )

        val_word_pool = load_words("val_word_pool", vals_words, nc.sync, "key_scale_pool")
        base_sb = sb.tile([P, T], F32, name="base_sb", tag="prior_pool")
        nc.sync.dma_start(base_sb[:], base)

        dquery_mx, gout_mx = quantize_pair("directions", (directions_raw[:, 0], directions_raw[:, 1]), nc.vector.tensor_copy)
        val_scales = sb.tile([P, SLOTS], U8, name="val_scales", align_bytes=64)
        nc.vector.tensor_copy(val_scales[:], val_scale_pool[:].indirect(offsets[:]))

        ea, neg_eb, both = wide("ea"), wide("neg_eb", "query2_raw"), wide("both", "directions_bf16")
        exp_ab = sb.tile([P, 2, 2, HALF], F32, name="exp_ab", align_bytes=64)
        for h in range(2):
            ab_bank = ps.tile([P, 2, HALF], F32, name="ab_bank%d" % h)
            product(ab_bank[:, 0, :], query_mx, key_words[:, halves[h]], key_scales[:, halves[h]])
            product(ab_bank[:, 1, :], query2_mx, key_words[:, halves[h]], key_scales[:, halves[h]])
            nc.scalar.activation(exp_ab[:, :, h, :], ab_bank[:], ACT.Exp)
        flat_prior = prior_bank[:].rearrange("p h i -> p (h i)")
        nc.vector.tensor_tensor(ea[:], exp_ab[:, 0].rearrange("p h i -> p (h i)"), flat_prior, ALU.mult)
        nc.vector.scalar_tensor_tensor(
            neg_eb[:], flat_prior, 1.0, exp_ab[:, 1].rearrange("p h i -> p (h i)"), ALU.subtract, ALU.mult
        )
        nc.vector.tensor_tensor(both[:], ea[:], neg_eb[:], ALU.subtract)

        ln_both, ln_ea = wide("ln_both"), wide("ln_ea")
        nc.scalar.activation(ln_ea[:], ea[:], ACT.Ln)
        nc.scalar.activation(ln_both[:], both[:], ACT.Ln)
        placed = sb.tile([P, T], F32, name="placed", tag="ea", align_bytes=64)
        nc.gpsimd.memset(placed[:], 0.0)

        val_words = sb.tile([P, SLOTS], U32, name="val_words", tag="query2_raw", align_bytes=64)
        nc.vector.tensor_copy(val_words[:], val_word_pool[:].indirect(offsets[:]))
        ta_bank = ps.tile([P, SLOTS], F32, name="ta_bank")
        product(ta_bank[:], dquery_mx, key_words[:], key_scales[:])
        c0_bank = ps.tile([P, SLOTS], F32, name="c0_bank")
        product(c0_bank[:], gout_mx, val_words[:], val_scales[:])

        neg_s = wide("neg_s", "key_scale_pool")
        neg_max, ln_r, ln_rp = column("neg_max"), wide("ln_r"), wide("ln_rp")
        nc.vector.tensor_scalar(neg_s[:], ln_both[:], neg_lam[:], None, ALU.mult, ALU.min, accum_out=neg_max[:])
        nc.vector.scalar_tensor_tensor(ln_rp[:], ln_both[:], lam_less_1[:], ln_ea[:], ALU.mult, ALU.add)
        nc.vector.tensor_tensor(ln_r[:], ln_ea[:], ln_both[:], ALU.subtract)

        p, p_sum, rp, r, curve = wide("p"), column("p_sum"), wide("rp"), wide("r"), wide("curve")
        nc.scalar.activation(p[:], neg_s[:], ACT.Exp, scale=-1.0, bias=neg_max[:], accum_out=p_sum[:])
        nc.scalar.activation(rp[:], ln_rp[:], ACT.Exp, bias=neg_max[:])
        nc.scalar.activation(r[:], ln_r[:], ACT.Exp)
        nc.scalar.activation(curve[:], r[:], ACT.Identity, scale=lam_less_1[:], bias=1.0)

        inv_sum, neg_c_sum, neg_c_mean = column("inv_sum"), column("neg_c_sum"), column("neg_c_mean")
        neg_pc, rpt, rpt_sum = wide("neg_pc"), wide("rpt"), column("rpt_sum")
        nc.vector.reciprocal(inv_sum[:], p_sum[:])
        nc.vector.scalar_tensor_tensor(neg_pc[:], c0_bank[:], -1.0, p[:], ALU.mult, ALU.mult, accum_out=neg_c_sum[:])
        nc.vector.scalar_tensor_tensor(rpt[:], ta_bank[:], 1.0, rp[:], ALU.mult, ALU.mult, accum_out=rpt_sum[:])
        nc.gpsimd.tensor_scalar(neg_c_mean[:], neg_c_sum[:], inv_sum[:], 0.0, ALU.mult, ALU.add)

        first, second, slope, shift = column("first"), column("second"), column("slope"), column("shift")
        nc.gpsimd.tensor_scalar(second[:], inv_sum[:], inv_sum[:], neg_lam2_512[:], ALU.mult, ALU.mult)
        nc.gpsimd.tensor_scalar(first[:], inv_sum[:], lam_512[:], 0.0, ALU.mult, ALU.add)
        nc.gpsimd.tensor_scalar(slope[:], rpt_sum[:], second[:], 0.0, ALU.mult, ALU.add)
        nc.gpsimd.tensor_scalar(shift[:], rpt_sum[:], second[:], neg_c_mean[:], ALU.mult, ALU.mult)

        rptc, rptc_sum = wide("rptc"), column("rptc_sum")
        nc.vector.scalar_tensor_tensor(rptc[:], c0_bank[:], neg_c_mean[:], rpt[:], ALU.add, ALU.mult, accum_out=rptc_sum[:])

        mean_term = wide("mean_term")
        nc.scalar.activation(mean_term[:], c0_bank[:], ACT.Identity, scale=slope[:], bias=shift[:])

        cov_term, own, shared = column("cov_term"), wide("own"), wide("shared")
        nc.vector.tensor_tensor(cov_term[:], rptc_sum[:], second[:], ALU.mult)
        nc.vector.scalar_tensor_tensor(own[:], rptc[:], first[:], curve[:], ALU.mult, ALU.mult)
        nc.vector.scalar_tensor_tensor(shared[:], mean_term[:], cov_term[:], rp[:], ALU.add, ALU.mult)
        nc.vector.tensor_tensor(placed[:].indirect(offsets[:]), own[:], shared[:], ALU.add)

        for c in range(len(OUT_EDGES) - 1):
            cols = slice(OUT_EDGES[c], OUT_EDGES[c + 1])
            result = sb.tile([P, cols.stop - cols.start], F32, name="result%d" % c)
            nc.vector.tensor_tensor(result[:], placed[:, cols], base_sb[:, cols], ALU.add)
            nc.sync.dma_start(out[:, cols], result[:])
